import numpy as np
import ml_dtypes


def mxq(x, axis, fmt="e4m3"):
    dtype, down = {"e4m3": (ml_dtypes.float8_e4m3fn, 7), "e5m2": (ml_dtypes.float8_e5m2, 14)}[fmt]
    v = np.moveaxis(np.asarray(x, np.float32).astype(ml_dtypes.bfloat16).astype(np.float64), axis, -1)
    blocks = v.reshape(v.shape[:-1] + (-1, 32))
    amax = np.abs(blocks).max(-1, keepdims=True)
    byte = np.maximum(np.where(amax > 0, np.frexp(amax)[1] - 1 + 127, 0) - down, 1)
    scale = np.exp2(byte - 127.0)
    codes = (blocks / scale).astype(np.float32).astype(dtype).astype(np.float64)
    return np.moveaxis((codes * scale).reshape(v.shape), -1, axis)


WIDE = False


def mx_kscale(k):
    if not WIDE:
        return np.ones(k)
    levels = np.array([10, -10, 5, -5, 0])
    if k % 512:
        return np.exp2(np.random.permutation(np.resize(levels, k // 32))).repeat(32)
    a = np.empty((k // 512, 16))
    for p in range(k // 512):
        a[p, :8] = np.random.permutation(np.resize(levels, 8))
        for g in range(8):
            far = levels[np.abs(levels - a[p, g]) >= 10]
            a[p, g + 8] = far[np.random.randint(len(far))]
    return np.exp2(a.ravel()).repeat(32)


def f64(x):
    return np.asarray(x).astype(np.float64)


def striped(idx):
    return np.tile(idx.reshape(-1, 16).T, (8, 1)).astype(np.uint16)


def unstriped(offs):
    return offs[:16].T.reshape(-1).astype(np.int64)


def silu(v):
    return v / (1.0 + np.exp(-np.maximum(v, -700.0)))


K, T, E, C, H, N = 512, 768, 12, 128, 512, 256


def by_expert(wq, xq):
    return np.concatenate([wq[e].T @ xq[:, e * C:(e + 1) * C] for e in range(E)], axis=1)


def setup_inputs():
    n = np.random.standard_normal
    s = mx_kscale(K)[:, None]
    u = mx_kscale(H)
    first = np.random.permutation(np.repeat(np.arange(E), T // E))
    second = (first + 1 + np.random.permutation(np.repeat(np.arange(E - 1), -(-T // (E - 1)))[:T])) % E
    while np.bincount(second, minlength=E).max() != T // E:
        load = np.bincount(second, minlength=E); hi, lo = int(load.argmax()), int(load.argmin())
        t = np.flatnonzero((second == hi) & (first != lo))[0]; second[t] = lo
    slot_token = np.empty(E * C, np.int64); pos = np.empty((2, T), np.int64); fill = np.zeros(E, np.int64)
    place = np.stack([np.random.permutation(C) for _ in range(E)])
    for r, deal in enumerate((first, second)):
        for t in np.random.permutation(T):
            e = deal[t]; j = e * C + place[e, fill[e]]; fill[e] += 1; slot_token[j] = t; pos[r, t] = j
    g = np.random.uniform(0.2, 0.8, T)
    return {
        "xT": (n((K, T)) * s).astype(np.float32),
        "w1": (n((E, K, H)) / np.sqrt(K) / s[None]).astype(np.float32),
        "w3": (n((E, K, H)) / np.sqrt(K) / s[None] * u[None, None, :]).astype(np.float32),
        "w2": (n((E, H, N)) / np.sqrt(H) / u[None, :, None]).astype(np.float32),
        "gate": np.stack([np.tile(g, (N, 1)), np.tile(1.0 - g, (N, 1))]).astype(np.float32),
        "offs": striped(slot_token),
        "pos1": striped(pos[0]),
        "pos2": striped(pos[1]),
    }


def reference(xT, w1, w3, w2, gate, offs, pos1, pos2):
    idx = unstriped(offs)
    xq = mxq(f64(xT)[:, idx], 0, "e4m3")
    h = silu(by_expert(mxq(f64(w1), 1, "e4m3"), xq))
    h = h * by_expert(mxq(f64(w3), 1, "e4m3"), xq)
    y = by_expert(mxq(f64(w2), 1, "e4m3"), mxq(h, 0, "e4m3"))
    return f64(gate[0]) * y[:, unstriped(pos1)] + f64(gate[1]) * y[:, unstriped(pos2)]

from contextlib import ExitStack

import concourse.mybir as mybir
from concourse.masks import make_identity

K, T, E, C, H, N = 512, 768, 12, 128, 512, 256
S = E * C
P = 128
PACK = 4
NB = N // P
FLOPS = 2 * S * (2 * K * H + H * N)

F32 = mybir.dt.float32
BF16 = mybir.dt.bfloat16
U32 = mybir.dt.uint32
U16 = mybir.dt.uint16
U8 = mybir.dt.uint8
FP8X4 = mybir.dt.float8_e4m3fn_x4
MULT = mybir.AluOpType.mult
ADD = mybir.AluOpType.add
SILU = mybir.ActivationFunctionType.Silu

LAG = 3
GATHER = 512
W1_ON_SCALAR = (1,)
W2_ON_VECTOR = ()
RAW13_BUFS = 10
RAW2_BUFS = 6


def tile_routed_moe_kernel(tc, xT, w1, w3, w2, gate, offs, pos1, pos2, out):
    nc = tc.nc
    w1_rows = w1.rearrange("e (p j) h -> e p j h", j=PACK)
    w3_rows = w3.rearrange("e (p j) h -> e p j h", j=PACK)
    w2_rows = w2.rearrange("e (p j) n -> e p j n", j=PACK)

    with ExitStack() as ctx:
        keep = ctx.enter_context(tc.tile_pool(name="keep", bufs=1))
        stage = ctx.enter_context(tc.tile_pool(name="stage", bufs=1))
        work = ctx.enter_context(tc.tile_pool(name="work", bufs=1))
        psum = ctx.enter_context(tc.psum_pool(name="psum", bufs=2))

        offs_t = keep.tile([P, S // 16], U16, name="offs_t")
        pos1_t = keep.tile([P, T // 16], U16, name="pos1_t")
        pos2_t = keep.tile([P, T // 16], U16, name="pos2_t")
        nc.sync.dma_start(offs_t[:], offs)

        x_raw = keep.tile([P, PACK, T], F32, name="x_raw")
        ident = keep.tile([P, P], F32, name="ident")

        x_scales = keep.tile([P, T], U8, name="x_scales", align_bytes=64)
        nc.gpsimd.memset(x_scales[:], 0)
        warm = keep.tile([P, 1], F32, name="warm")
        warm_out = keep.tile([P, 1], F32, name="warm_out")
        nc.gpsimd.memset(warm[:], 0.0)
        nc.scalar.activation(warm_out[:], warm[:], SILU)
        make_identity(nc, ident[:])

        y_all = [keep.tile([P, S], F32, name=f"y_all{b}") for b in range(NB)]

        raw1, raw3, raw2, gates = {}, {}, {}, {}

        def load(s):
            if s < E:
                raw1[s] = stage.tile([P, PACK, H], F32, name="w1_raw", tag="raw13", bufs=RAW13_BUFS)
                nc.sync.dma_start(raw1[s][:], w1_rows[s])
                if s == 0:
                    nc.sync.dma_start(x_raw[:], xT.rearrange("(p j) t -> p j t", j=PACK))
                if s == 2:
                    nc.sync.dma_start(pos1_t[:], pos1)
                    nc.sync.dma_start(pos2_t[:], pos2)
                raw3[s] = stage.tile([P, PACK, H], F32, name="w3_raw", tag="raw13", bufs=RAW13_BUFS)
                nc.sync.dma_start(raw3[s][:], w3_rows[s])
            e = s - LAG
            if 0 <= e < E:
                raw2[e] = stage.tile([P, PACK, N], F32, name="w2_raw", tag="raw2", bufs=RAW2_BUFS)
                nc.sync.dma_start(raw2[e][:], w2_rows[e])
            if e == E - 1:
                for b in range(NB):
                    for r in range(2):
                        gates[r, b] = stage.tile([P, T], F32, name="gate_t", tag="raw2", bufs=RAW2_BUFS)
                        nc.sync.dma_start(gates[r, b][:], gate[r, b * P : (b + 1) * P, :])

        def plain_interleave(copy, dst, src):
            copy(
                dst.rearrange("p (c i) t -> p c t i", i=4),
                src.rearrange("p t (c i) -> p c t i", i=4),
            )

        def permuted_interleave(copy, dst, src, m0, m1):
            copy(
                dst[:].rearrange("p (t m j) -> p m j t", t=PACK, j=PACK)[:, m0:m1],
                src[:].rearrange("p j (m t) -> p m j t", t=PACK)[:, m0:m1],
            )

        def quantize(codes, scales, values):
            nc.vector.quantize_mx(codes.bitcast(FP8X4), scales, values)

        x_grp = keep.tile([P, T, PACK], BF16, name="x_grp", align_bytes=64)
        x_codes = keep.tile([P, T], U32, name="x_codes", align_bytes=64)
        slot_codes = keep.tile([P, S], U32, name="slot_codes", align_bytes=64)
        slot_scales = keep.tile([P, S], U8, name="slot_scales", align_bytes=64)

        def tokens():
            plain_interleave(nc.vector.tensor_copy, x_grp[:, 0:512, :], x_raw[:, :, 0:512])
            plain_interleave(nc.scalar.copy, x_grp[:, 512:T, :], x_raw[:, :, 512:T])
            for lo, hi in ((0, 512), (512, T)):
                quantize(x_codes[:, lo:hi], x_scales[:, lo:hi], x_grp[:, lo:hi, :].rearrange("p c t -> p (c t)"))
            for lo in range(0, S, GATHER):
                entries = offs_t[:, lo // 16 : (lo + GATHER) // 16]
                nc.vector.tensor_copy(slot_codes[:, lo : lo + GATHER], x_codes[:].indirect(entries))
                nc.vector.tensor_copy(slot_scales[:, lo : lo + GATHER], x_scales[:].indirect(entries))

        def matmul(acc, w_codes, w_scales, m, codes, scales):
            nc.tensor.matmul_mx(
                out=acc,
                lhsT=w_codes[:, m * P : (m + 1) * P].bitcast(FP8X4),
                lhsT_scale=w_scales[:, m * P : (m + 1) * P],
                rhs=codes.bitcast(FP8X4),
                rhs_scale=scales,
                start=True,
                stop=True,
            )

        grp1, grp3, grp2, q2, ab, act, hid, hq, ys = {}, {}, {}, {}, {}, {}, {}, {}, {}

        def product(e, name, grp):
            codes = work.tile([P, H], U32, name=f"{name}_codes", tag="codes13", bufs=4, align_bytes=64)
            scales = work.tile([P, H], U8, name=f"{name}_scales", tag="scales13", bufs=4, align_bytes=64)
            quantize(codes[:], scales[:], grp[:])
            acc = psum.tile([P, PACK, C], F32, name=f"{name}_acc")
            for t in range(PACK):
                matmul(acc[:, t, :], codes, scales, t, slot_codes[:, e * C : (e + 1) * C], slot_scales[:, e * C : (e + 1) * C])
            return acc

        def gather_times_gate(b, r, lo, hi):
            pos = (pos1_t, pos2_t)[r]
            term = work.tile([P, hi - lo], F32, name=f"term{r}", tag=f"term{b}{r}{lo}", bufs=1)
            nc.vector.tensor_tensor(
                term[:], y_all[b][:].indirect(pos[:, lo // 16 : hi // 16]), gates[r, b][:, lo:hi], MULT
            )
            return term

        def add_on_tensor(b, first, second, lo, hi, tag):
            acc = psum.tile([P, hi - lo], F32, name="sum_acc", tag=tag)
            nc.tensor.matmul(acc[:], ident[:], first, start=True, stop=False)
            nc.tensor.matmul(acc[:], ident[:], second, start=False, stop=True)
            total = work.tile([P, hi - lo], F32, name="total", tag=f"total{b}{lo}", bufs=1)
            nc.scalar.copy(total[:], acc[:])
            nc.sync.dma_start(out[b * P : (b + 1) * P, lo:hi], total[:])

        def combine():
            first = gather_times_gate(0, 0, 0, T)
            second = gather_times_gate(0, 1, 0, T)
            add_on_tensor(0, first[:, 0:384], second[:, 0:384], 0, 384, "w1_acc")
            add_on_tensor(0, first[:, 384:T], second[:, 384:T], 384, T, "w3_acc")
            first = gather_times_gate(1, 0, 0, T)
            second = gather_times_gate(1, 1, 0, 384)
            add_on_tensor(1, first[:, 0:384], second[:], 0, 384, "w1_acc")
            second = gather_times_gate(1, 1, 384, T)
            total = work.tile([P, T - 384], F32, name="total_last", bufs=1)
            nc.vector.tensor_tensor(total[:], first[:, 384:T], second[:], ADD)
            nc.sync.dma_start(out[P : 2 * P, 384:T], total[:])

        AHEAD = 2
        for s in range(AHEAD):
            load(s)
        for s in range(E + LAG + 1):
            load(s + AHEAD)
            if s < E:
                grp1[s] = work.tile([P, PACK * H], BF16, name="grp1", tag="grp13", bufs=4, align_bytes=64)
                permuted_interleave(nc.scalar.copy if s in W1_ON_SCALAR else nc.vector.tensor_copy, grp1[s], raw1[s], 0, P)
                if s == 0:
                    tokens()
                grp3[s] = work.tile([P, PACK * H], BF16, name="grp3", tag="grp13", bufs=4, align_bytes=64)
                cut = 0 if s < E - 1 else 80
                if cut:
                    permuted_interleave(nc.vector.tensor_copy, grp3[s], raw3[s], 0, cut)
                permuted_interleave(nc.scalar.copy, grp3[s], raw3[s], cut, P)
            e = s - LAG - 1
            if e >= 0:
                codes = work.tile([P, N], U32, name="codes2", bufs=2, align_bytes=64)
                scales = work.tile([P, N], U8, name="scales2", bufs=2, align_bytes=64)
                step = N if e < E - 1 else P
                for lo in range(0, N, step):
                    part = slice(lo, lo + step)
                    quantize(codes[:, part], scales[:, part], grp2[e][:, part, :].rearrange("p c t -> p (c t)"))
                h_codes, h_scales = hq[e]
                for b in range(NB):
                    if e % 2 == 0 or e == E - 1:
                        ys[b] = psum.tile([P, 2 * C], F32, name=f"y_acc{b}")
                    matmul(ys[b][:, (e % 2) * C : (e % 2 + 1) * C], codes, scales, b, h_codes[:], h_scales[:])
            if 1 <= s <= E:
                p = s - 1
                a_acc, b_acc = ab[p]
                act = work.tile([P, C, PACK], F32, name="act", bufs=2)
                nc.scalar.activation(act[:], a_acc[:].rearrange("p t c -> p c t"), SILU)
                hid = work.tile([P, C, PACK], BF16, name="hid", bufs=2, align_bytes=64)
                nc.vector.tensor_tensor(hid[:], b_acc[:].rearrange("p t c -> p c t"), act[:], MULT)
            if s < E:
                a_new = product(s, "w1", grp1[s])
            if 1 <= s <= E:
                h_codes = work.tile([P, C], U32, name="h_codes", bufs=4, align_bytes=64)
                h_scales = work.tile([P, C], U8, name="h_scales", bufs=4, align_bytes=64)
                quantize(h_codes[:], h_scales[:], hid[:].rearrange("p c t -> p (c t)"))
                hq[s - 1] = (h_codes, h_scales)
            if s < E:
                ab[s] = (a_new, product(s, "w3", grp3[s]))
            e2 = s - LAG
            if 0 <= e2 < E:
                grp2[e2] = work.tile([P, N, PACK], BF16, name="grp2", bufs=3, align_bytes=64)
                cut = N if e2 in W2_ON_VECTOR else (0 if e2 < E - 1 else P)
                if cut:
                    plain_interleave(nc.vector.tensor_copy, grp2[e2][:, 0:cut, :], raw2[e2][:, :, 0:cut])
                if cut < N:
                    plain_interleave(nc.scalar.copy, grp2[e2][:, cut:N, :], raw2[e2][:, :, cut:N])
            if e >= 0 and (e % 2 == 1 or e >= E - 2):
                first_e = e - 1 if e < E - 2 else e
                part = slice((first_e % 2) * C, (e % 2 + 1) * C)
                cols = slice(first_e * C, (e + 1) * C)
                nc.scalar.copy(y_all[0][:, cols], ys[0][:, part])
                nc.scalar.copy(y_all[1][:, cols], ys[1][:, part])
        combine()
